import numpy as np
import ml_dtypes


def mxq(x, axis, fmt="e4m3"):
    dtype, down = {"e4m3": (ml_dtypes.float8_e4m3fn, 7), "e5m2": (ml_dtypes.float8_e5m2, 14)}[fmt]
    v = np.moveaxis(np.asarray(x, np.float32).astype(ml_dtypes.bfloat16).astype(np.float64), axis, -1)
    blocks = v.reshape(v.shape[:-1] + (-1, 32))
    amax = np.abs(blocks).max(-1, keepdims=True)
    byte = np.maximum(np.where(amax > 0, np.frexp(amax)[1] - 1 + 127, 0) - down, 1)
    scale = np.exp2(byte - 127.0)
    codes = (blocks / scale).astype(np.float32).astype(dtype).astype(np.float64)
    return np.moveaxis((codes * scale).reshape(v.shape), -1, axis)


WIDE = False


def mx_kscale(k):
    if not WIDE:
        return np.ones(k)
    levels = np.array([10, -10, 5, -5, 0])
    if k % 512:
        return np.exp2(np.random.permutation(np.resize(levels, k // 32))).repeat(32)
    a = np.empty((k // 512, 16))
    for p in range(k // 512):
        a[p, :8] = np.random.permutation(np.resize(levels, 8))
        for g in range(8):
            far = levels[np.abs(levels - a[p, g]) >= 10]
            a[p, g + 8] = far[np.random.randint(len(far))]
    return np.exp2(a.ravel()).repeat(32)


def f64(x):
    return np.asarray(x).astype(np.float64)


def striped(idx):
    return np.tile(idx.reshape(-1, 16).T, (8, 1)).astype(np.uint16)


def unstriped(offs):
    return offs[:16].T.reshape(-1).astype(np.int64)


E2M1 = np.array([0.0, 0.5, 1.0, 1.5, 2.0, 3.0, 4.0, 6.0, -0.0, -0.5, -1.0, -1.5, -2.0, -3.0, -4.0, -6.0])


def pack_weight(w, fmt):
    k, n = w.shape
    w = f64(np.asarray(w, np.float32).astype(ml_dtypes.bfloat16)).reshape(k // 32, 32, n)
    amax = np.abs(w).max(1)
    if fmt == "e4m3":
        byte = np.frexp(amax)[1] - 1 + 127 - 7
    else:
        mant, ex = np.frexp(amax / 6.0)
        byte = np.where(mant > 0.5, ex, ex - 1) + 127
    byte = np.clip(np.where(amax > 0, byte, 1), 1, 254)
    scaled = (w * np.exp2(127.0 - byte)[:, None, :]).reshape(k, n).astype(np.float32)
    by_word = np.ascontiguousarray(scaled.reshape(k // 512, 128, 4, n).transpose(0, 1, 3, 2))
    if fmt == "e4m3":
        words = by_word.astype(ml_dtypes.float8_e4m3fn).view(np.uint8)
    else:
        c = by_word.astype(ml_dtypes.float4_e2m1fn).view(np.uint8) & 0xF
        words = (c[..., 0::2] | (c[..., 1::2] << 4)).reshape(k // 512, 128, 2 * n)
    return np.ascontiguousarray(words), np.ascontiguousarray(byte.astype(np.uint8).reshape(k // 512, 16, n))


def unpack_weight(words, scales, fmt):
    g, _, n = scales.shape
    words = np.ascontiguousarray(words).reshape(g, 128, n, -1)
    if fmt == "e4m3":
        vals = words.view(ml_dtypes.float8_e4m3fn).astype(np.float64)
    else:
        nib = np.empty((g, 128, n, 4), np.uint8)
        nib[..., 0::2] = words & 0xF
        nib[..., 1::2] = words >> 4
        vals = E2M1[nib]
    vals = vals * np.repeat(np.exp2(scales.astype(np.float64) - 127.0), 8, axis=1)[..., None]
    return vals.transpose(0, 1, 3, 2).reshape(g * 512, n)


def gelu(v):
    return 0.5 * v * (1.0 + np.tanh(np.sqrt(2.0 / np.pi) * (v + 0.044715 * v**3)))


K, K2, H, N, T, S = 1024, 512, 1024, 384, 2048, 1024

def setup_inputs():
    n = np.random.standard_normal
    s = mx_kscale(K)[:, None]
    s2 = mx_kscale(K2)[:, None]
    u = mx_kscale(H)[:, None]
    d = {}
    d["tab_words"], d["tab_scales"] = pack_weight(n((K, T)) * s, "e4m3")
    d["offs"] = striped(np.random.permutation(T)[:S])
    d["xs_words"], d["xs_scales"] = pack_weight(n((K2, S)) * s2, "e4m3")
    d["w1"] = (n((K, H)) / K ** 0.5 / s * u.T).astype(np.float32)
    d["w2"] = (n((K2, H)) / K2 ** 0.5 / s2 * u.T).astype(np.float32)
    d["w3_words"], d["w3_scales"] = pack_weight(n((K2, H)) / K2 ** 0.5 / s2 * u.T, "e2m1")
    d["w4_words"], d["w4_scales"] = pack_weight(n((H, N)) / H ** 0.5 / u, "e4m3")
    return d

def reference(tab_words, tab_scales, offs, xs_words, xs_scales, w1, w2, w3_words, w3_scales, w4_words, w4_scales):
    v = unpack_weight(tab_words, tab_scales, "e4m3")[:, unstriped(offs)]
    xs = unpack_weight(xs_words, xs_scales, "e4m3")
    w3 = unpack_weight(w3_words, w3_scales, "e2m1")
    w4 = unpack_weight(w4_words, w4_scales, "e4m3")
    a = mxq(f64(w1), 0, "e4m3").T @ v
    b = mxq(f64(w2), 0, "e4m3").T @ xs
    d = w3.T @ xs
    z = np.abs(a - b) + np.abs(a - d)
    out = w4.T @ mxq(z, 0, "e4m3")
    return out

@@ -1,0 +1,252 @@
+from contextlib import ExitStack
+
+import concourse.mybir as mybir
+
+K, K2, H, N, T, S = 1024, 512, 1024, 384, 2048, 1024
+FLOPS = 2 * S * (K * H + 2 * K2 * H + H * N)
+
+F32 = mybir.dt.float32
+BF16 = mybir.dt.bfloat16
+I32 = mybir.dt.int32
+U32 = mybir.dt.uint32
+U16 = mybir.dt.uint16
+U8 = mybir.dt.uint8
+FP8X4 = mybir.dt.float8_e4m3fn_x4
+FP4X4 = mybir.dt.float4_e2m1fn_x4
+ALU = mybir.AluOpType
+ACT = mybir.ActivationFunctionType
+
+P = 128
+PACK = 4
+KP = P * PACK
+TOK = 128
+UNITS_PER_BLOCK = S // TOK
+BLOCKS = H // KP
+OUT_TOK = 256
+DIRECT = (5, 10, 15)
+
+
+def tile_list_film_bubble_predictor_kernel(
+    tc, tab_words, tab_scales, offs, xs_words, xs_scales, w1, w2, w3_words, w3_scales, w4_words, w4_scales, out
+):
+    nc = tc.nc
+    with ExitStack() as ctx:
+        keep = ctx.enter_context(tc.tile_pool(name="keep", bufs=1))
+        work = ctx.enter_context(tc.tile_pool(name="work", bufs=4))
+        psum = ctx.enter_context(tc.psum_pool(name="psum", bufs=2))
+
+        offsets = keep.tile([P, S // 16], U16, name="offsets")
+        nc.sync.dma_start(offsets[:], offs)
+
+        def plane(name, width, engine):
+            tile = keep.tile([P, width], U8, name=name, align_bytes=64)
+            engine.memset(tile[:].bitcast(I32), 0)
+            return tile
+
+        def load_plane(queue, tile, scales):
+            passes = scales.shape[0]
+            for q in range(4):
+                queue.dma_start(
+                    out=tile[32 * q : 32 * q + 4 * passes, :].bitcast(I32),
+                    in_=scales[:, 4 * q : 4 * q + 4, :].bitcast(I32),
+                )
+
+        def load_words(name, words):
+            tile = keep.tile([P, words.shape[1]], I32, name=name, align_bytes=64)
+            nc.sync.dma_start(out=tile[:], in_=words.rearrange("p c i -> p (c i)").bitcast(I32))
+            return tile
+
+        def load_weight(name, rows, b):
+            tile = keep.tile([P, PACK, KP], F32, name=name)
+            nc.sync.dma_start(out=tile[:], in_=rows[:, b * KP : (b + 1) * KP].rearrange("(p j) c -> p j c", j=PACK))
+            return tile
+
+        tab_plane = plane("tab_plane", T, nc.gpsimd)
+        w3_plane_raw = plane("w3_plane_raw", H, nc.vector)
+        xs_plane = plane("xs_plane", S, nc.vector)
+        w4_plane = plane("w4_plane", N, nc.vector)
+
+        tab = [None, None]
+        raw = {}
+        tab[0] = load_words("tab0", tab_words[0])
+        load_plane(nc.sync, tab_plane, tab_scales)
+        raw[0, 0] = load_weight("raw00", w1[0:KP, :], 0)
+        raw[1, 0] = load_weight("raw10", w1[KP:K, :], 0)
+        load_plane(nc.sync, w3_plane_raw, w3_scales)
+        w3_raw = keep.tile([P, H // 2], I32, name="w3_raw", align_bytes=64)
+        nc.sync.dma_start(out=w3_raw[:], in_=w3_words[0].bitcast(I32))
+        tab[1] = load_words("tab1", tab_words[1])
+        load_plane(nc.sync, xs_plane, xs_scales)
+        xs = load_words("xs", xs_words[0])
+        raw[2, 0] = load_weight("raw20", w2, 0)
+        raw[0, 1] = load_weight("raw01", w1[0:KP, :], 1)
+        raw[1, 1] = load_weight("raw11", w1[KP:K, :], 1)
+        raw[2, 1] = load_weight("raw21", w2, 1)
+        load_plane(nc.sync, w4_plane, w4_scales)
+        w4 = [load_words(f"w4_{a}", w4_words[a]) for a in range(BLOCKS)]
+
+        w3 = keep.tile([P, 2 * H], U8, name="w3", align_bytes=64)
+        w3_plane = keep.tile([P, H], U8, name="w3_plane", align_bytes=64)
+        nc.vector.tensor_copy(
+            out=w3[:].bitcast(U16).rearrange("p (b t m) -> p b m t", b=BLOCKS, t=PACK),
+            in_=w3_raw[:].bitcast(U16).rearrange("p (b m t) -> p b m t", b=BLOCKS, t=PACK),
+        )
+        nc.vector.tensor_copy(
+            out=w3_plane[:].rearrange("p (b t m) -> p b m t", b=BLOCKS, t=PACK),
+            in_=w3_plane_raw[:].rearrange("p (b m t) -> p b m t", b=BLOCKS, t=PACK),
+        )
+
+        v = [keep.tile([P, S], U32, name=f"v{a}", align_bytes=64) for a in range(2)]
+        v_plane = keep.tile([P, S], U8, name="v_plane", align_bytes=64)
+
+        def gather(dst, window, lo, hi):
+            nc.vector.tensor_copy(dst[:, lo:hi], window.indirect(offsets[:, lo // 16 : hi // 16]))
+
+        codes, planes, rounded = {}, {}, {}
+
+        def round_weight(i, b, on_vector):
+            sign = -1.0 if i < 2 else 1.0
+            tile = keep.tile([P, PACK, P, PACK], BF16, name=f"rounded{i}{b}", align_bytes=64)
+            rounded[i, b] = tile
+            dst = tile[:].rearrange("p t m j -> p m j t")
+            src = raw[i, b][:].rearrange("p j (m t) -> p m j t", t=PACK)
+            if on_vector > 0:
+                nc.vector.tensor_scalar(dst[:, :on_vector], src[:, :on_vector], sign, None, ALU.mult)
+            if on_vector < P:
+                nc.scalar.activation(dst[:, on_vector:], src[:, on_vector:], ACT.Copy, scale=sign)
+
+        def quantize_weight(i, b, pieces):
+            codes[i, b] = keep.tile([P, KP], U32, name=f"codes{i}{b}", align_bytes=64)
+            planes[i, b] = keep.tile([P, KP], U8, name=f"plane{i}{b}", align_bytes=64)
+            flat = rounded[i, b][:].rearrange("p t m j -> p (t m j)")
+            w = KP // pieces
+            for h in range(pieces):
+                nc.vector.quantize_mx(
+                    out=codes[i, b][:, h * w : (h + 1) * w].bitcast(FP8X4),
+                    scales=planes[i, b][:, h * w : (h + 1) * w],
+                    in_=flat[:, h * w * PACK : (h + 1) * w * PACK],
+                )
+
+        gather(v[0], tab[0][:].bitcast(U32), 0, S)
+        gather(v_plane, tab_plane[:], 0, S)
+        round_weight(0, 0, 0)
+        quantize_weight(0, 0, 1)
+        round_weight(1, 0, 0)
+        quantize_weight(1, 0, 1)
+        for lo, hi in ((0, S // 4), (S // 4, S // 2), (S // 2, S)):
+            gather(v[1], tab[1][:].bitcast(U32), lo, hi)
+        round_weight(2, 0, 80)
+        quantize_weight(2, 0, 2)
+
+        def passes(kind, b, t, tok):
+            cols = slice(t * P, (t + 1) * P)
+            if kind == "a":
+                return [
+                    (codes[i, b][:, cols].bitcast(FP8X4), planes[i, b][:, cols],
+                     v[i][:, tok].bitcast(FP8X4), v_plane[4 * i :, tok])
+                    for i in range(2)
+                ]
+            moving = (xs[:, tok].bitcast(FP8X4), xs_plane[:, tok])
+            if kind == "b":
+                return [(codes[2, b][:, cols].bitcast(FP8X4), planes[2, b][:, cols]) + moving]
+            c0 = b * KP + t * P
+            return [(w3[:, 2 * c0 : 2 * (c0 + P)].bitcast(FP4X4), w3_plane[:, c0 : c0 + P]) + moving]
+
+        def product(kinds, u, tag):
+            b, s = divmod(u, UNITS_PER_BLOCK)
+            tok = slice(s * TOK, (s + 1) * TOK)
+            bank = psum.tile([P, PACK, TOK], F32, name=tag, tag=tag)
+            for t in range(PACK):
+                group = [step for kind in kinds for step in passes(kind, b, t, tok)]
+                for g, (lhsT, lhsT_scale, rhs, rhs_scale) in enumerate(group):
+                    nc.tensor.matmul_mx(out=bank[:, t, :], lhsT=lhsT, lhsT_scale=lhsT_scale, rhs=rhs,
+                                        rhs_scale=rhs_scale, start=(g == 0), stop=(g == len(group) - 1))
+            return bank[:].rearrange("p t n -> p n t")
+
+        minus_a, diff, mag = {}, {}, {}
+        z = [keep.tile([P, S * PACK], BF16, name=f"z{b}", align_bytes=64) for b in range(BLOCKS)]
+        z_codes = [keep.tile([P, S], U32, name=f"z_codes{b}", align_bytes=64) for b in range(BLOCKS)]
+        z_plane = [keep.tile([P, S], U8, name=f"z_plane{b}", align_bytes=64) for b in range(BLOCKS)]
+
+        def stage_a(u):
+            if u in DIRECT:
+                return
+            bank = product("a", u, "bank_a")
+            minus_a[u] = work.tile([P, TOK, PACK], F32, name="minus_a", bufs=6)
+            nc.scalar.copy(minus_a[u][:], bank)
+
+        def stage_diff(u):
+            mag[u] = work.tile([P, 2, TOK, PACK], F32, name="mag")
+            if u in DIRECT:
+                for h, kind in enumerate("db"):
+                    bank = product("a" + kind, u, "bank_" + kind)
+                    nc.scalar.activation(mag[u][:, h], bank, ACT.Abs)
+                return
+            diff[u] = work.tile([P, 2, TOK, PACK], F32, name="diff", bufs=5)
+            for h, kind in enumerate("db"):
+                bank = product(kind, u, "bank_" + kind)
+                nc.vector.tensor_tensor(diff[u][:, h], bank, minus_a[u][:], ALU.add)
+
+        def stage_abs(u):
+            if u in DIRECT:
+                return
+            src = diff[u][:].rearrange("p h n t -> p (h n t)")
+            dst = mag[u][:].rearrange("p h n t -> p (h n t)")
+            width = KP if u < 4 else 2 * KP
+            for c in range(0, 2 * KP, width):
+                nc.scalar.activation(dst[:, c : c + width], src[:, c : c + width], ACT.Abs)
+
+        def stage_sum(u):
+            b, s = divmod(u, UNITS_PER_BLOCK)
+            flat = mag[u][:].rearrange("p h n t -> p h (n t)")
+            nc.vector.tensor_tensor(z[b][:, s * KP : (s + 1) * KP], flat[:, 0], flat[:, 1], ALU.add)
+
+        def quantize_z(b, lo, hi):
+            nc.vector.quantize_mx(out=z_codes[b][:, lo:hi].bitcast(FP8X4), scales=z_plane[b][:, lo:hi],
+                                  in_=z[b][:, lo * PACK : hi * PACK])
+
+        def stage_out(lo, hi):
+            width = hi - lo
+            result = work.tile([P, N // P, width], F32, name="result", bufs=3)
+            per_bank = min(N // P, KP // width)
+            for n0 in range(0, N // P, per_bank):
+                count = min(per_bank, N // P - n0)
+                bank = psum.tile([P, count, width], F32, name="bank_o", tag="bank_o")
+                for n in range(n0, n0 + count):
+                    cols = slice(n * P, (n + 1) * P)
+                    for b in range(BLOCKS):
+                        nc.tensor.matmul_mx(out=bank[:, n - n0, :], lhsT=w4[b][:, cols].bitcast(FP8X4),
+                                            lhsT_scale=w4_plane[4 * b :, cols], rhs=z_codes[b][:, lo:hi].bitcast(FP8X4),
+                                            rhs_scale=z_plane[b][:, lo:hi], start=(b == 0), stop=(b == BLOCKS - 1))
+                if width == OUT_TOK:
+                    nc.scalar.copy(result[:, n0 : n0 + count, :], bank[:])
+                else:
+                    nc.vector.tensor_copy(result[:, n0 : n0 + count, :], bank[:])
+            nc.sync.dma_start(out=out[:, lo:hi].rearrange("(n p) j -> p n j", p=P), in_=result[:])
+
+        units = BLOCKS * UNITS_PER_BLOCK
+        later = {2: (0, 64), 4: (1, 64), 5: (2, 64)}
+        for step in range(-1, units + 3):
+            if 0 <= step + 1 < units:
+                stage_a(step + 1)
+            if 0 <= step < units:
+                stage_diff(step)
+            if 0 <= step - 1 < units:
+                stage_abs(step - 1)
+            if step in later:
+                round_weight(later[step][0], 1, later[step][1])
+            if 0 <= step - 2 < units:
+                stage_sum(step - 2)
+            if step - 1 in later:
+                quantize_weight(later[step - 1][0], 1, 1)
+            u = step - 3
+            if 0 <= u < units:
+                b, s = divmod(u, UNITS_PER_BLOCK)
+                if b == 0 and s % 4 == 3:
+                    quantize_z(b, (s - 3) * TOK, (s + 1) * TOK)
+                if b == 1 and s % 2 == 1 and s < 6:
+                    quantize_z(b, (s - 1) * TOK, (s + 1) * TOK)
+                    stage_out((s - 1) * TOK, (s + 1) * TOK)
+                if b == 1 and s >= 6:
+                    quantize_z(b, s * TOK, (s + 1) * TOK)
+                    stage_out(s * TOK, (s + 1) * TOK)

@@ -18,12 +18,23 @@ ACT = mybir.ActivationFunctionType
 
 P = 128
 PACK = 4
-KP = P * PACK
-TOK = 128
-UNITS_PER_BLOCK = S // TOK
-BLOCKS = H // KP
-OUT_TOK = 256
-DIRECT = (5, 10, 15)
+PASS = P * PACK
+BANK = 512
+BLOCKS = H // PASS
+TOK = BANK // PACK
+PER_BLOCK = S // TOK
+UNITS = BLOCKS * PER_BLOCK
+
+FUSED = (5, 10, 15)
+SPLIT_ABS = 4
+SINGLE_FROM = UNITS - 2
+
+W1_LO, W1_HI, W2 = 0, 1, 2
+LATE_ON_VECTOR = 40
+LATE_ROUNDING = {2: W1_LO, 3: W1_HI, 5: W2}
+MINUS_A_REUSES = {6: (W1_HI, 1)}
+DIFF_REUSES = {4: (W1_LO, 1), 7: (W2, 1)}
+DIFF_PAIR = 2
 
 
 def tile_list_film_bubble_predictor_kernel(
@@ -32,22 +43,21 @@ def tile_list_film_bubble_predictor_kernel(
     nc = tc.nc
     with ExitStack() as ctx:
         keep = ctx.enter_context(tc.tile_pool(name="keep", bufs=1))
-        work = ctx.enter_context(tc.tile_pool(name="work", bufs=4))
+        work = ctx.enter_context(tc.tile_pool(name="work", bufs=3))
         psum = ctx.enter_context(tc.psum_pool(name="psum", bufs=2))
 
         offsets = keep.tile([P, S // 16], U16, name="offsets")
         nc.sync.dma_start(offsets[:], offs)
 
-        def plane(name, width, engine):
+        def zeroed_plane(name, width, engine):
             tile = keep.tile([P, width], U8, name=name, align_bytes=64)
             engine.memset(tile[:].bitcast(I32), 0)
             return tile
 
-        def load_plane(queue, tile, scales):
-            passes = scales.shape[0]
+        def load_plane(tile, scales):
             for q in range(4):
-                queue.dma_start(
-                    out=tile[32 * q : 32 * q + 4 * passes, :].bitcast(I32),
+                nc.sync.dma_start(
+                    out=tile[32 * q : 32 * q + 4 * scales.shape[0], :].bitcast(I32),
                     in_=scales[:, 4 * q : 4 * q + 4, :].bitcast(I32),
                 )
 
@@ -56,197 +66,209 @@ def tile_list_film_bubble_predictor_kernel(
             nc.sync.dma_start(out=tile[:], in_=words.rearrange("p c i -> p (c i)").bitcast(I32))
             return tile
 
-        def load_weight(name, rows, b):
-            tile = keep.tile([P, PACK, KP], F32, name=name)
-            nc.sync.dma_start(out=tile[:], in_=rows[:, b * KP : (b + 1) * KP].rearrange("(p j) c -> p j c", j=PACK))
-            return tile
+        weight_rows = {W1_LO: w1[0:PASS, :], W1_HI: w1[PASS:K, :], W2: w2}
+        staged = {}
 
-        tab_plane = plane("tab_plane", T, nc.gpsimd)
-        w3_plane_raw = plane("w3_plane_raw", H, nc.vector)
-        xs_plane = plane("xs_plane", S, nc.vector)
-        w4_plane = plane("w4_plane", N, nc.vector)
+        def staging_tag(key):
+            return "staged%d%d" % key
 
-        tab = [None, None]
-        raw = {}
-        tab[0] = load_words("tab0", tab_words[0])
-        load_plane(nc.sync, tab_plane, tab_scales)
-        raw[0, 0] = load_weight("raw00", w1[0:KP, :], 0)
-        raw[1, 0] = load_weight("raw10", w1[KP:K, :], 0)
-        load_plane(nc.sync, w3_plane_raw, w3_scales)
+        def load_weight(i, c):
+            tile = keep.tile([P, PACK, PASS], F32, name=staging_tag((i, c)), tag=staging_tag((i, c)))
+            rows = weight_rows[i][:, c * PASS : (c + 1) * PASS]
+            nc.sync.dma_start(out=tile[:], in_=rows.rearrange("(p j) r -> p j r", j=PACK))
+            staged[i, c] = tile
+
+        tab_plane = zeroed_plane("tab_plane", T, nc.gpsimd)
+        w3_plane_raw = zeroed_plane("w3_plane_raw", H, nc.vector)
+        xs_plane = zeroed_plane("xs_plane", S, nc.vector)
+        w4_plane = zeroed_plane("w4_plane", N, nc.vector)
+
+        tab_lo = load_words("tab_lo", tab_words[0])
+        load_plane(tab_plane, tab_scales)
+        load_weight(W1_LO, 0)
+        load_weight(W1_HI, 0)
+        load_plane(w3_plane_raw, w3_scales)
         w3_raw = keep.tile([P, H // 2], I32, name="w3_raw", align_bytes=64)
         nc.sync.dma_start(out=w3_raw[:], in_=w3_words[0].bitcast(I32))
-        tab[1] = load_words("tab1", tab_words[1])
-        load_plane(nc.sync, xs_plane, xs_scales)
+        tab_hi = load_words("tab_hi", tab_words[1])
+        load_plane(xs_plane, xs_scales)
         xs = load_words("xs", xs_words[0])
-        raw[2, 0] = load_weight("raw20", w2, 0)
-        raw[0, 1] = load_weight("raw01", w1[0:KP, :], 1)
-        raw[1, 1] = load_weight("raw11", w1[KP:K, :], 1)
-        raw[2, 1] = load_weight("raw21", w2, 1)
-        load_plane(nc.sync, w4_plane, w4_scales)
-        w4 = [load_words(f"w4_{a}", w4_words[a]) for a in range(BLOCKS)]
+        load_weight(W2, 0)
+        load_weight(W1_LO, 1)
+        load_weight(W1_HI, 1)
+        load_plane(w4_plane, w4_scales)
+        w4 = [load_words("w4_%d" % c, w4_words[c]) for c in range(BLOCKS)]
+        load_weight(W2, 1)
 
         w3 = keep.tile([P, 2 * H], U8, name="w3", align_bytes=64)
         w3_plane = keep.tile([P, H], U8, name="w3_plane", align_bytes=64)
-        nc.vector.tensor_copy(
-            out=w3[:].bitcast(U16).rearrange("p (b t m) -> p b m t", b=BLOCKS, t=PACK),
-            in_=w3_raw[:].bitcast(U16).rearrange("p (b m t) -> p b m t", b=BLOCKS, t=PACK),
-        )
-        nc.vector.tensor_copy(
-            out=w3_plane[:].rearrange("p (b t m) -> p b m t", b=BLOCKS, t=PACK),
-            in_=w3_plane_raw[:].rearrange("p (b m t) -> p b m t", b=BLOCKS, t=PACK),
-        )
+        for dst, src in ((w3[:].bitcast(U16), w3_raw[:].bitcast(U16)), (w3_plane[:], w3_plane_raw[:])):
+            nc.vector.tensor_copy(
+                out=dst.rearrange("p (c t m) -> p c m t", c=BLOCKS, t=PACK),
+                in_=src.rearrange("p (c m t) -> p c m t", c=BLOCKS, t=PACK),
+            )
 
-        v = [keep.tile([P, S], U32, name=f"v{a}", align_bytes=64) for a in range(2)]
+        v = [keep.tile([P, S], U32, name="v%d" % a, align_bytes=64) for a in range(K // PASS)]
         v_plane = keep.tile([P, S], U8, name="v_plane", align_bytes=64)
 
         def gather(dst, window, lo, hi):
             nc.vector.tensor_copy(dst[:, lo:hi], window.indirect(offsets[:, lo // 16 : hi // 16]))
 
-        codes, planes, rounded = {}, {}, {}
+        rounded, codes, planes = {}, {}, {}
 
-        def round_weight(i, b, on_vector):
-            sign = -1.0 if i < 2 else 1.0
-            tile = keep.tile([P, PACK, P, PACK], BF16, name=f"rounded{i}{b}", align_bytes=64)
-            rounded[i, b] = tile
-            dst = tile[:].rearrange("p t m j -> p m j t")
-            src = raw[i, b][:].rearrange("p j (m t) -> p m j t", t=PACK)
+        def round_weight(i, c, on_vector):
+            sign = 1.0 if i == W2 else -1.0
+            rounded[i, c] = keep.tile([P, PACK, P, PACK], BF16, name="rounded%d%d" % (i, c), align_bytes=64)
+            dst = rounded[i, c][:].rearrange("p t m j -> p m j t")
+            src = staged[i, c][:].rearrange("p j (m t) -> p m j t", t=PACK)
             if on_vector > 0:
                 nc.vector.tensor_scalar(dst[:, :on_vector], src[:, :on_vector], sign, None, ALU.mult)
             if on_vector < P:
                 nc.scalar.activation(dst[:, on_vector:], src[:, on_vector:], ACT.Copy, scale=sign)
 
-        def quantize_weight(i, b, pieces):
-            codes[i, b] = keep.tile([P, KP], U32, name=f"codes{i}{b}", align_bytes=64)
-            planes[i, b] = keep.tile([P, KP], U8, name=f"plane{i}{b}", align_bytes=64)
-            flat = rounded[i, b][:].rearrange("p t m j -> p (t m j)")
-            w = KP // pieces
-            for h in range(pieces):
+        def quantize_weight(i, c, pieces=1):
+            codes[i, c] = keep.tile([P, PASS], U32, name="codes%d%d" % (i, c), align_bytes=64)
+            planes[i, c] = keep.tile([P, PASS], U8, name="plane%d%d" % (i, c), align_bytes=64)
+            flat = rounded[i, c][:].rearrange("p t m j -> p (t m j)")
+            width = PASS // pieces
+            for lo in range(0, PASS, width):
                 nc.vector.quantize_mx(
-                    out=codes[i, b][:, h * w : (h + 1) * w].bitcast(FP8X4),
-                    scales=planes[i, b][:, h * w : (h + 1) * w],
-                    in_=flat[:, h * w * PACK : (h + 1) * w * PACK],
+                    out=codes[i, c][:, lo : lo + width].bitcast(FP8X4),
+                    scales=planes[i, c][:, lo : lo + width],
+                    in_=flat[:, lo * PACK : (lo + width) * PACK],
                 )
 
-        gather(v[0], tab[0][:].bitcast(U32), 0, S)
+        gather(v[0], tab_lo[:].bitcast(U32), 0, S)
         gather(v_plane, tab_plane[:], 0, S)
-        round_weight(0, 0, 0)
-        quantize_weight(0, 0, 1)
-        round_weight(1, 0, 0)
-        quantize_weight(1, 0, 1)
+        for i in (W1_LO, W1_HI):
+            round_weight(i, 0, 0)
+            quantize_weight(i, 0)
         for lo, hi in ((0, S // 4), (S // 4, S // 2), (S // 2, S)):
-            gather(v[1], tab[1][:].bitcast(U32), lo, hi)
-        round_weight(2, 0, 80)
-        quantize_weight(2, 0, 2)
+            gather(v[1], tab_hi[:].bitcast(U32), lo, hi)
+        round_weight(W2, 0, P)
+        quantize_weight(W2, 0, pieces=2)
 
-        def passes(kind, b, t, tok):
+        def passes(kind, c, t, tok):
             cols = slice(t * P, (t + 1) * P)
             if kind == "a":
                 return [
-                    (codes[i, b][:, cols].bitcast(FP8X4), planes[i, b][:, cols],
+                    (codes[i, c][:, cols].bitcast(FP8X4), planes[i, c][:, cols],
                      v[i][:, tok].bitcast(FP8X4), v_plane[4 * i :, tok])
-                    for i in range(2)
+                    for i in (W1_LO, W1_HI)
                 ]
             moving = (xs[:, tok].bitcast(FP8X4), xs_plane[:, tok])
             if kind == "b":
-                return [(codes[2, b][:, cols].bitcast(FP8X4), planes[2, b][:, cols]) + moving]
-            c0 = b * KP + t * P
-            return [(w3[:, 2 * c0 : 2 * (c0 + P)].bitcast(FP4X4), w3_plane[:, c0 : c0 + P]) + moving]
+                return [(codes[W2, c][:, cols].bitcast(FP8X4), planes[W2, c][:, cols]) + moving]
+            first = c * PASS + t * P
+            return [(w3[:, 2 * first : 2 * (first + P)].bitcast(FP4X4), w3_plane[:, first : first + P]) + moving]
 
         def product(kinds, u, tag):
-            b, s = divmod(u, UNITS_PER_BLOCK)
+            c, s = divmod(u, PER_BLOCK)
             tok = slice(s * TOK, (s + 1) * TOK)
             bank = psum.tile([P, PACK, TOK], F32, name=tag, tag=tag)
-            for t in range(PACK):
-                group = [step for kind in kinds for step in passes(kind, b, t, tok)]
-                for g, (lhsT, lhsT_scale, rhs, rhs_scale) in enumerate(group):
-                    nc.tensor.matmul_mx(out=bank[:, t, :], lhsT=lhsT, lhsT_scale=lhsT_scale, rhs=rhs,
-                                        rhs_scale=rhs_scale, start=(g == 0), stop=(g == len(group) - 1))
+            by_slice = [[ops for kind in kinds for ops in passes(kind, c, t, tok)] for t in range(PACK)]
+            depth = len(by_slice[0])
+            for g in range(depth):
+                for t in range(PACK):
+                    lhsT, lhsT_scale, rhs, rhs_scale = by_slice[t][g]
+                    nc.tensor.matmul_mx(
+                        out=bank[:, t, :], lhsT=lhsT, lhsT_scale=lhsT_scale, rhs=rhs, rhs_scale=rhs_scale,
+                        start=(g == 0 and t == 0), stop=(g == depth - 1 and t == PACK - 1),
+                    )
             return bank[:].rearrange("p t n -> p n t")
 
         minus_a, diff, mag = {}, {}, {}
-        z = [keep.tile([P, S * PACK], BF16, name=f"z{b}", align_bytes=64) for b in range(BLOCKS)]
-        z_codes = [keep.tile([P, S], U32, name=f"z_codes{b}", align_bytes=64) for b in range(BLOCKS)]
-        z_plane = [keep.tile([P, S], U8, name=f"z_plane{b}", align_bytes=64) for b in range(BLOCKS)]
+        z = [keep.tile([P, S * PACK], BF16, name="z%d" % c, align_bytes=64) for c in range(BLOCKS)]
+        z_codes = [keep.tile([P, S], U32, name="z_codes%d" % c, align_bytes=64) for c in range(BLOCKS)]
+        z_plane = [keep.tile([P, S], U8, name="z_plane%d" % c, align_bytes=64) for c in range(BLOCKS)]
 
-        def stage_a(u):
-            if u in DIRECT:
+        def copy_minus_a(u):
+            if u in FUSED:
                 return
             bank = product("a", u, "bank_a")
-            minus_a[u] = work.tile([P, TOK, PACK], F32, name="minus_a", bufs=6)
+            if u in MINUS_A_REUSES:
+                minus_a[u] = keep.tile([P, TOK, PACK], F32, name="minus_a", tag=staging_tag(MINUS_A_REUSES[u]))
+            else:
+                minus_a[u] = work.tile([P, TOK, PACK], F32, name="minus_a", bufs=5)
             nc.scalar.copy(minus_a[u][:], bank)
 
-        def stage_diff(u):
-            mag[u] = work.tile([P, 2, TOK, PACK], F32, name="mag")
-            if u in DIRECT:
+        def differences(u):
+            mag[u] = work.tile([P, 2, TOK, PACK], F32, name="mag", bufs=SPLIT_ABS)
+            if u in FUSED:
                 for h, kind in enumerate("db"):
-                    bank = product("a" + kind, u, "bank_" + kind)
-                    nc.scalar.activation(mag[u][:, h], bank, ACT.Abs)
+                    nc.scalar.activation(mag[u][:, h], product("a" + kind, u, "bank_" + kind), ACT.Abs)
                 return
-            diff[u] = work.tile([P, 2, TOK, PACK], F32, name="diff", bufs=5)
+            if u == DIFF_PAIR:
+                pair = keep.tile([P, 2, 2, TOK, PACK], F32, name="diff_pair", tag=staging_tag((W2, 0)))
+                diff[u], diff[u + 1] = pair[:, 0], pair[:, 1]
+            elif u in DIFF_REUSES:
+                diff[u] = keep.tile([P, 2, TOK, PACK], F32, name="diff", tag=staging_tag(DIFF_REUSES[u]))[:]
+            elif u not in diff:
+                diff[u] = work.tile([P, 2, TOK, PACK], F32, name="diff")[:]
             for h, kind in enumerate("db"):
-                bank = product(kind, u, "bank_" + kind)
-                nc.vector.tensor_tensor(diff[u][:, h], bank, minus_a[u][:], ALU.add)
+                nc.vector.tensor_tensor(diff[u][:, h], product(kind, u, "bank_" + kind), minus_a[u][:], ALU.add)
 
-        def stage_abs(u):
-            if u in DIRECT:
+        def absolute_values(u):
+            if u in FUSED:
                 return
-            src = diff[u][:].rearrange("p h n t -> p (h n t)")
+            src = diff[u].rearrange("p h n t -> p (h n t)")
             dst = mag[u][:].rearrange("p h n t -> p (h n t)")
-            width = KP if u < 4 else 2 * KP
-            for c in range(0, 2 * KP, width):
-                nc.scalar.activation(dst[:, c : c + width], src[:, c : c + width], ACT.Abs)
+            width = BANK if u < SPLIT_ABS else 2 * BANK
+            for lo in range(0, 2 * BANK, width):
+                nc.scalar.activation(dst[:, lo : lo + width], src[:, lo : lo + width], ACT.Abs)
 
-        def stage_sum(u):
-            b, s = divmod(u, UNITS_PER_BLOCK)
+        def add_and_round(u):
+            c, s = divmod(u, PER_BLOCK)
             flat = mag[u][:].rearrange("p h n t -> p h (n t)")
-            nc.vector.tensor_tensor(z[b][:, s * KP : (s + 1) * KP], flat[:, 0], flat[:, 1], ALU.add)
+            nc.vector.tensor_tensor(z[c][:, s * BANK : (s + 1) * BANK], flat[:, 0], flat[:, 1], ALU.add)
 
-        def quantize_z(b, lo, hi):
-            nc.vector.quantize_mx(out=z_codes[b][:, lo:hi].bitcast(FP8X4), scales=z_plane[b][:, lo:hi],
-                                  in_=z[b][:, lo * PACK : hi * PACK])
+        def quantize_z(c, lo, hi):
+            nc.vector.quantize_mx(
+                out=z_codes[c][:, lo:hi].bitcast(FP8X4), scales=z_plane[c][:, lo:hi], in_=z[c][:, lo * PACK : hi * PACK]
+            )
 
-        def stage_out(lo, hi):
+        def scores(lo, hi):
             width = hi - lo
-            result = work.tile([P, N // P, width], F32, name="result", bufs=3)
-            per_bank = min(N // P, KP // width)
-            for n0 in range(0, N // P, per_bank):
-                count = min(per_bank, N // P - n0)
-                bank = psum.tile([P, count, width], F32, name="bank_o", tag="bank_o")
+            tiles = N // P
+            result = work.tile([P, tiles, width], F32, name="result")
+            per_bank = min(tiles, BANK // width)
+            for n0 in range(0, tiles, per_bank):
+                count = min(per_bank, tiles - n0)
+                bank = psum.tile([P, count, width], F32, name="bank_out", tag="bank_out")
                 for n in range(n0, n0 + count):
                     cols = slice(n * P, (n + 1) * P)
-                    for b in range(BLOCKS):
-                        nc.tensor.matmul_mx(out=bank[:, n - n0, :], lhsT=w4[b][:, cols].bitcast(FP8X4),
-                                            lhsT_scale=w4_plane[4 * b :, cols], rhs=z_codes[b][:, lo:hi].bitcast(FP8X4),
-                                            rhs_scale=z_plane[b][:, lo:hi], start=(b == 0), stop=(b == BLOCKS - 1))
-                if width == OUT_TOK:
+                    for c in range(BLOCKS):
+                        nc.tensor.matmul_mx(
+                            out=bank[:, n - n0, :], lhsT=w4[c][:, cols].bitcast(FP8X4), lhsT_scale=w4_plane[4 * c :, cols],
+                            rhs=z_codes[c][:, lo:hi].bitcast(FP8X4), rhs_scale=z_plane[c][:, lo:hi],
+                            start=(c == 0), stop=(c == BLOCKS - 1),
+                        )
+                if width > TOK:
                     nc.scalar.copy(result[:, n0 : n0 + count, :], bank[:])
                 else:
                     nc.vector.tensor_copy(result[:, n0 : n0 + count, :], bank[:])
             nc.sync.dma_start(out=out[:, lo:hi].rearrange("(n p) j -> p n j", p=P), in_=result[:])
 
-        units = BLOCKS * UNITS_PER_BLOCK
-        later = {2: (0, 64), 4: (1, 64), 5: (2, 64)}
-        for step in range(-1, units + 3):
-            if 0 <= step + 1 < units:
-                stage_a(step + 1)
-            if 0 <= step < units:
-                stage_diff(step)
-            if 0 <= step - 1 < units:
-                stage_abs(step - 1)
-            if step in later:
-                round_weight(later[step][0], 1, later[step][1])
-            if 0 <= step - 2 < units:
-                stage_sum(step - 2)
-            if step - 1 in later:
-                quantize_weight(later[step - 1][0], 1, 1)
+        for step in range(-1, UNITS + 3):
+            if step + 1 < UNITS:
+                copy_minus_a(step + 1)
+            if 0 <= step < UNITS:
+                differences(step)
+            if 0 <= step - 1 < UNITS:
+                absolute_values(step - 1)
+            if step in LATE_ROUNDING:
+                round_weight(LATE_ROUNDING[step], 1, LATE_ON_VECTOR)
+            if 0 <= step - 2 < UNITS:
+                add_and_round(step - 2)
+            if step - 1 in LATE_ROUNDING:
+                quantize_weight(LATE_ROUNDING[step - 1], 1)
             u = step - 3
-            if 0 <= u < units:
-                b, s = divmod(u, UNITS_PER_BLOCK)
-                if b == 0 and s % 4 == 3:
-                    quantize_z(b, (s - 3) * TOK, (s + 1) * TOK)
-                if b == 1 and s % 2 == 1 and s < 6:
-                    quantize_z(b, (s - 1) * TOK, (s + 1) * TOK)
-                    stage_out((s - 1) * TOK, (s + 1) * TOK)
-                if b == 1 and s >= 6:
-                    quantize_z(b, s * TOK, (s + 1) * TOK)
-                    stage_out(s * TOK, (s + 1) * TOK)
+            if u >= 0:
+                c, s = divmod(u, PER_BLOCK)
+                end = (s + 1) * TOK
+                if c == 0 and end % (S // 2) == 0:
+                    quantize_z(c, end - S // 2, end)
+                if c == 1 and (u >= SINGLE_FROM or s % 2 == 1):
+                    first = end - (TOK if u >= SINGLE_FROM else 2 * TOK)
+                    quantize_z(c, first, end)
+                    scores(first, end)

from contextlib import ExitStack

import concourse.mybir as mybir

K, K2, H, N, T, S = 1024, 512, 1024, 384, 2048, 1024
FLOPS = 2 * S * (K * H + 2 * K2 * H + H * N)

F32 = mybir.dt.float32
BF16 = mybir.dt.bfloat16
I32 = mybir.dt.int32
U32 = mybir.dt.uint32
U16 = mybir.dt.uint16
U8 = mybir.dt.uint8
FP8X4 = mybir.dt.float8_e4m3fn_x4
FP4X4 = mybir.dt.float4_e2m1fn_x4
ALU = mybir.AluOpType
ACT = mybir.ActivationFunctionType

P = 128
PACK = 4
PASS = P * PACK
BANK = 512
BLOCKS = H // PASS
TOK = BANK // PACK
PER_BLOCK = S // TOK
UNITS = BLOCKS * PER_BLOCK

FUSED = (5, 10, 15)
SPLIT_ABS = 4
SINGLE_FROM = UNITS - 2

W1_LO, W1_HI, W2 = 0, 1, 2
LATE_ON_VECTOR = 40
LATE_ROUNDING = {2: W1_LO, 3: W1_HI, 5: W2}
MINUS_A_REUSES = {6: (W1_HI, 1)}
DIFF_REUSES = {4: (W1_LO, 1), 7: (W2, 1)}
DIFF_PAIR = 2


def tile_list_film_bubble_predictor_kernel(
    tc, tab_words, tab_scales, offs, xs_words, xs_scales, w1, w2, w3_words, w3_scales, w4_words, w4_scales, out
):
    nc = tc.nc
    with ExitStack() as ctx:
        keep = ctx.enter_context(tc.tile_pool(name="keep", bufs=1))
        work = ctx.enter_context(tc.tile_pool(name="work", bufs=3))
        psum = ctx.enter_context(tc.psum_pool(name="psum", bufs=2))

        offsets = keep.tile([P, S // 16], U16, name="offsets")
        nc.sync.dma_start(offsets[:], offs)

        def zeroed_plane(name, width, engine):
            tile = keep.tile([P, width], U8, name=name, align_bytes=64)
            engine.memset(tile[:].bitcast(I32), 0)
            return tile

        def load_plane(tile, scales):
            for q in range(4):
                nc.sync.dma_start(
                    out=tile[32 * q : 32 * q + 4 * scales.shape[0], :].bitcast(I32),
                    in_=scales[:, 4 * q : 4 * q + 4, :].bitcast(I32),
                )

        def load_words(name, words):
            tile = keep.tile([P, words.shape[1]], I32, name=name, align_bytes=64)
            nc.sync.dma_start(out=tile[:], in_=words.rearrange("p c i -> p (c i)").bitcast(I32))
            return tile

        weight_rows = {W1_LO: w1[0:PASS, :], W1_HI: w1[PASS:K, :], W2: w2}
        staged = {}

        def staging_tag(key):
            return "staged%d%d" % key

        def load_weight(i, c):
            tile = keep.tile([P, PACK, PASS], F32, name=staging_tag((i, c)), tag=staging_tag((i, c)))
            rows = weight_rows[i][:, c * PASS : (c + 1) * PASS]
            nc.sync.dma_start(out=tile[:], in_=rows.rearrange("(p j) r -> p j r", j=PACK))
            staged[i, c] = tile

        tab_plane = zeroed_plane("tab_plane", T, nc.gpsimd)
        w3_plane_raw = zeroed_plane("w3_plane_raw", H, nc.vector)
        xs_plane = zeroed_plane("xs_plane", S, nc.vector)
        w4_plane = zeroed_plane("w4_plane", N, nc.vector)

        tab_lo = load_words("tab_lo", tab_words[0])
        load_plane(tab_plane, tab_scales)
        load_weight(W1_LO, 0)
        load_weight(W1_HI, 0)
        load_plane(w3_plane_raw, w3_scales)
        w3_raw = keep.tile([P, H // 2], I32, name="w3_raw", align_bytes=64)
        nc.sync.dma_start(out=w3_raw[:], in_=w3_words[0].bitcast(I32))
        tab_hi = load_words("tab_hi", tab_words[1])
        load_plane(xs_plane, xs_scales)
        xs = load_words("xs", xs_words[0])
        load_weight(W2, 0)
        load_weight(W1_LO, 1)
        load_weight(W1_HI, 1)
        load_plane(w4_plane, w4_scales)
        w4 = [load_words("w4_%d" % c, w4_words[c]) for c in range(BLOCKS)]
        load_weight(W2, 1)

        w3 = keep.tile([P, 2 * H], U8, name="w3", align_bytes=64)
        w3_plane = keep.tile([P, H], U8, name="w3_plane", align_bytes=64)
        for dst, src in ((w3[:].bitcast(U16), w3_raw[:].bitcast(U16)), (w3_plane[:], w3_plane_raw[:])):
            nc.vector.tensor_copy(
                out=dst.rearrange("p (c t m) -> p c m t", c=BLOCKS, t=PACK),
                in_=src.rearrange("p (c m t) -> p c m t", c=BLOCKS, t=PACK),
            )

        v = [keep.tile([P, S], U32, name="v%d" % a, align_bytes=64) for a in range(K // PASS)]
        v_plane = keep.tile([P, S], U8, name="v_plane", align_bytes=64)

        def gather(dst, window, lo, hi):
            nc.vector.tensor_copy(dst[:, lo:hi], window.indirect(offsets[:, lo // 16 : hi // 16]))

        rounded, codes, planes = {}, {}, {}

        def round_weight(i, c, on_vector):
            sign = 1.0 if i == W2 else -1.0
            rounded[i, c] = keep.tile([P, PACK, P, PACK], BF16, name="rounded%d%d" % (i, c), align_bytes=64)
            dst = rounded[i, c][:].rearrange("p t m j -> p m j t")
            src = staged[i, c][:].rearrange("p j (m t) -> p m j t", t=PACK)
            if on_vector > 0:
                nc.vector.tensor_scalar(dst[:, :on_vector], src[:, :on_vector], sign, None, ALU.mult)
            if on_vector < P:
                nc.scalar.activation(dst[:, on_vector:], src[:, on_vector:], ACT.Copy, scale=sign)

        def quantize_weight(i, c, pieces=1):
            codes[i, c] = keep.tile([P, PASS], U32, name="codes%d%d" % (i, c), align_bytes=64)
            planes[i, c] = keep.tile([P, PASS], U8, name="plane%d%d" % (i, c), align_bytes=64)
            flat = rounded[i, c][:].rearrange("p t m j -> p (t m j)")
            width = PASS // pieces
            for lo in range(0, PASS, width):
                nc.vector.quantize_mx(
                    out=codes[i, c][:, lo : lo + width].bitcast(FP8X4),
                    scales=planes[i, c][:, lo : lo + width],
                    in_=flat[:, lo * PACK : (lo + width) * PACK],
                )

        gather(v[0], tab_lo[:].bitcast(U32), 0, S)
        gather(v_plane, tab_plane[:], 0, S)
        for i in (W1_LO, W1_HI):
            round_weight(i, 0, 0)
            quantize_weight(i, 0)
        for lo, hi in ((0, S // 4), (S // 4, S // 2), (S // 2, S)):
            gather(v[1], tab_hi[:].bitcast(U32), lo, hi)
        round_weight(W2, 0, P)
        quantize_weight(W2, 0, pieces=2)

        def passes(kind, c, t, tok):
            cols = slice(t * P, (t + 1) * P)
            if kind == "a":
                return [
                    (codes[i, c][:, cols].bitcast(FP8X4), planes[i, c][:, cols],
                     v[i][:, tok].bitcast(FP8X4), v_plane[4 * i :, tok])
                    for i in (W1_LO, W1_HI)
                ]
            moving = (xs[:, tok].bitcast(FP8X4), xs_plane[:, tok])
            if kind == "b":
                return [(codes[W2, c][:, cols].bitcast(FP8X4), planes[W2, c][:, cols]) + moving]
            first = c * PASS + t * P
            return [(w3[:, 2 * first : 2 * (first + P)].bitcast(FP4X4), w3_plane[:, first : first + P]) + moving]

        def product(kinds, u, tag):
            c, s = divmod(u, PER_BLOCK)
            tok = slice(s * TOK, (s + 1) * TOK)
            bank = psum.tile([P, PACK, TOK], F32, name=tag, tag=tag)
            by_slice = [[ops for kind in kinds for ops in passes(kind, c, t, tok)] for t in range(PACK)]
            depth = len(by_slice[0])
            for g in range(depth):
                for t in range(PACK):
                    lhsT, lhsT_scale, rhs, rhs_scale = by_slice[t][g]
                    nc.tensor.matmul_mx(
                        out=bank[:, t, :], lhsT=lhsT, lhsT_scale=lhsT_scale, rhs=rhs, rhs_scale=rhs_scale,
                        start=(g == 0 and t == 0), stop=(g == depth - 1 and t == PACK - 1),
                    )
            return bank[:].rearrange("p t n -> p n t")

        minus_a, diff, mag = {}, {}, {}
        z = [keep.tile([P, S * PACK], BF16, name="z%d" % c, align_bytes=64) for c in range(BLOCKS)]
        z_codes = [keep.tile([P, S], U32, name="z_codes%d" % c, align_bytes=64) for c in range(BLOCKS)]
        z_plane = [keep.tile([P, S], U8, name="z_plane%d" % c, align_bytes=64) for c in range(BLOCKS)]

        def copy_minus_a(u):
            if u in FUSED:
                return
            bank = product("a", u, "bank_a")
            if u in MINUS_A_REUSES:
                minus_a[u] = keep.tile([P, TOK, PACK], F32, name="minus_a", tag=staging_tag(MINUS_A_REUSES[u]))
            else:
                minus_a[u] = work.tile([P, TOK, PACK], F32, name="minus_a", bufs=5)
            nc.scalar.copy(minus_a[u][:], bank)

        def differences(u):
            mag[u] = work.tile([P, 2, TOK, PACK], F32, name="mag", bufs=SPLIT_ABS)
            if u in FUSED:
                for h, kind in enumerate("db"):
                    nc.scalar.activation(mag[u][:, h], product("a" + kind, u, "bank_" + kind), ACT.Abs)
                return
            if u == DIFF_PAIR:
                pair = keep.tile([P, 2, 2, TOK, PACK], F32, name="diff_pair", tag=staging_tag((W2, 0)))
                diff[u], diff[u + 1] = pair[:, 0], pair[:, 1]
            elif u in DIFF_REUSES:
                diff[u] = keep.tile([P, 2, TOK, PACK], F32, name="diff", tag=staging_tag(DIFF_REUSES[u]))[:]
            elif u not in diff:
                diff[u] = work.tile([P, 2, TOK, PACK], F32, name="diff")[:]
            for h, kind in enumerate("db"):
                nc.vector.tensor_tensor(diff[u][:, h], product(kind, u, "bank_" + kind), minus_a[u][:], ALU.add)

        def absolute_values(u):
            if u in FUSED:
                return
            src = diff[u].rearrange("p h n t -> p (h n t)")
            dst = mag[u][:].rearrange("p h n t -> p (h n t)")
            width = BANK if u < SPLIT_ABS else 2 * BANK
            for lo in range(0, 2 * BANK, width):
                nc.scalar.activation(dst[:, lo : lo + width], src[:, lo : lo + width], ACT.Abs)

        def add_and_round(u):
            c, s = divmod(u, PER_BLOCK)
            flat = mag[u][:].rearrange("p h n t -> p h (n t)")
            nc.vector.tensor_tensor(z[c][:, s * BANK : (s + 1) * BANK], flat[:, 0], flat[:, 1], ALU.add)

        def quantize_z(c, lo, hi):
            nc.vector.quantize_mx(
                out=z_codes[c][:, lo:hi].bitcast(FP8X4), scales=z_plane[c][:, lo:hi], in_=z[c][:, lo * PACK : hi * PACK]
            )

        def scores(lo, hi):
            width = hi - lo
            tiles = N // P
            result = work.tile([P, tiles, width], F32, name="result")
            per_bank = min(tiles, BANK // width)
            for n0 in range(0, tiles, per_bank):
                count = min(per_bank, tiles - n0)
                bank = psum.tile([P, count, width], F32, name="bank_out", tag="bank_out")
                for n in range(n0, n0 + count):
                    cols = slice(n * P, (n + 1) * P)
                    for c in range(BLOCKS):
                        nc.tensor.matmul_mx(
                            out=bank[:, n - n0, :], lhsT=w4[c][:, cols].bitcast(FP8X4), lhsT_scale=w4_plane[4 * c :, cols],
                            rhs=z_codes[c][:, lo:hi].bitcast(FP8X4), rhs_scale=z_plane[c][:, lo:hi],
                            start=(c == 0), stop=(c == BLOCKS - 1),
                        )
                if width > TOK:
                    nc.scalar.copy(result[:, n0 : n0 + count, :], bank[:])
                else:
                    nc.vector.tensor_copy(result[:, n0 : n0 + count, :], bank[:])
            nc.sync.dma_start(out=out[:, lo:hi].rearrange("(n p) j -> p n j", p=P), in_=result[:])

        for step in range(-1, UNITS + 3):
            if step + 1 < UNITS:
                copy_minus_a(step + 1)
            if 0 <= step < UNITS:
                differences(step)
            if 0 <= step - 1 < UNITS:
                absolute_values(step - 1)
            if step in LATE_ROUNDING:
                round_weight(LATE_ROUNDING[step], 1, LATE_ON_VECTOR)
            if 0 <= step - 2 < UNITS:
                add_and_round(step - 2)
            if step - 1 in LATE_ROUNDING:
                quantize_weight(LATE_ROUNDING[step - 1], 1)
            u = step - 3
            if u >= 0:
                c, s = divmod(u, PER_BLOCK)
                end = (s + 1) * TOK
                if c == 0 and end % (S // 2) == 0:
                    quantize_z(c, end - S // 2, end)
                if c == 1 and (u >= SINGLE_FROM or s % 2 == 1):
                    first = end - (TOK if u >= SINGLE_FROM else 2 * TOK)
                    quantize_z(c, first, end)
                    scores(first, end)
